import numpy as np
import ml_dtypes


def mxq(x, axis, fmt="e4m3"):
    dtype, down = {"e4m3": (ml_dtypes.float8_e4m3fn, 7), "e5m2": (ml_dtypes.float8_e5m2, 14)}[fmt]
    v = np.moveaxis(np.asarray(x, np.float32).astype(ml_dtypes.bfloat16).astype(np.float64), axis, -1)
    blocks = v.reshape(v.shape[:-1] + (-1, 32))
    amax = np.abs(blocks).max(-1, keepdims=True)
    byte = np.maximum(np.where(amax > 0, np.frexp(amax)[1] - 1 + 127, 0) - down, 1)
    scale = np.exp2(byte - 127.0)
    codes = (blocks / scale).astype(np.float32).astype(dtype).astype(np.float64)
    return np.moveaxis((codes * scale).reshape(v.shape), -1, axis)


WIDE = False


def mx_kscale(k):
    if not WIDE:
        return np.ones(k)
    levels = np.array([10, -10, 5, -5, 0])
    if k % 512:
        return np.exp2(np.random.permutation(np.resize(levels, k // 32))).repeat(32)
    a = np.empty((k // 512, 16))
    for p in range(k // 512):
        a[p, :8] = np.random.permutation(np.resize(levels, 8))
        for g in range(8):
            far = levels[np.abs(levels - a[p, g]) >= 10]
            a[p, g + 8] = far[np.random.randint(len(far))]
    return np.exp2(a.ravel()).repeat(32)


def f64(x):
    return np.asarray(x).astype(np.float64)


def striped(idx):
    return np.tile(np.asarray(idx).reshape(-1, 16).T, (8, 1)).astype(np.uint16)


def unstriped(offs):
    return offs[:16].T.reshape(-1).astype(np.int64)


E2M1 = np.array([0.0, 0.5, 1.0, 1.5, 2.0, 3.0, 4.0, 6.0, -0.0, -0.5, -1.0, -1.5, -2.0, -3.0, -4.0, -6.0])


def pack_weight(w, fmt):
    k, n = w.shape
    w = f64(np.asarray(w, np.float32).astype(ml_dtypes.bfloat16)).reshape(k // 32, 32, n)
    amax = np.abs(w).max(1)
    if fmt == "e4m3":
        byte = np.frexp(amax)[1] - 1 + 127 - 7
    else:
        mant, ex = np.frexp(amax / 6.0)
        byte = np.where(mant > 0.5, ex, ex - 1) + 127
    byte = np.clip(np.where(amax > 0, byte, 1), 1, 254)
    scaled = (w * np.exp2(127.0 - byte)[:, None, :]).reshape(k, n).astype(np.float32)
    by_word = np.ascontiguousarray(scaled.reshape(k // 512, 128, 4, n).transpose(0, 1, 3, 2))
    if fmt == "e4m3":
        words = by_word.astype(ml_dtypes.float8_e4m3fn).view(np.uint8)
    else:
        c = by_word.astype(ml_dtypes.float4_e2m1fn).view(np.uint8) & 0xF
        words = (c[..., 0::2] | (c[..., 1::2] << 4)).reshape(k // 512, 128, 2 * n)
    return np.ascontiguousarray(words), np.ascontiguousarray(byte.astype(np.uint8).reshape(k // 512, 16, n))


def unpack_weight(words, scales, fmt):
    g, _, n = scales.shape
    words = np.ascontiguousarray(words).reshape(g, 128, n, -1)
    if fmt == "e4m3":
        vals = words.view(ml_dtypes.float8_e4m3fn).astype(np.float64)
    else:
        nib = np.empty((g, 128, n, 4), np.uint8)
        nib[..., 0::2] = words & 0xF
        nib[..., 1::2] = words >> 4
        vals = E2M1[nib]
    vals = vals * np.repeat(np.exp2(scales.astype(np.float64) - 127.0), 8, axis=1)[..., None]
    return vals.transpose(0, 1, 3, 2).reshape(g * 512, n)


def bf(x):
    return np.asarray(x, np.float32).astype(ml_dtypes.bfloat16)


def planes(Y):
    r, m = Y.shape
    b = f64(bf(Y)).reshape(r // 32, 32, m)
    amax = np.abs(b).max(1)
    byte = np.clip(np.where(amax > 0, np.frexp(amax)[1] - 1 + 127 - 7, 1), 1, 254)
    codes = (b * np.exp2(127.0 - byte)[:, None, :]).reshape(r, m).astype(np.float32).astype(ml_dtypes.float8_e4m3fn).view(np.uint8)
    words = codes.reshape(r // 512, 128, 4, m).transpose(0, 1, 3, 2)
    return np.ascontiguousarray(words), np.ascontiguousarray(byte.astype(np.uint8).reshape(r // 512, 16, m))


K, T, J, N = 1024, 2048, 512, 512


def setup_inputs():
    n = np.random.standard_normal
    idx = np.random.permutation(T)[:J]
    idx2 = np.random.permutation(T)[:J]
    fk = mx_kscale(K)
    wap = pack_weight(n((K, N)) * 1 / np.sqrt(K) * fk[:, None], "e2m1")
    wbp = pack_weight(n((K, N)) * 1 / np.sqrt(K) * fk[:, None], "e4m3")
    return {
        "xt": (n((K, T)) * np.random.uniform(0.3, 1.7, (1, T)) / fk[:, None]).astype(np.float32),
        "wa_words": wap[0],
        "wa_scales": wap[1],
        "wb_words": wbp[0],
        "wb_scales": wbp[1],
        "bi": (np.random.uniform(-1.0, 1.0, (1, N))).astype(np.float32),
        "offs": striped(idx),
        "offs2": striped(idx2),
    }


def reference(xt, wa_words, wa_scales, wb_words, wb_scales, bi, offs, offs2):
    idx = unstriped(offs)
    idx2 = unstriped(offs2)
    wau = unpack_weight(wa_words, wa_scales, "e2m1")
    wbu = unpack_weight(wb_words, wb_scales, "e4m3")
    xtidxq = mxq(f64(xt)[:, idx], 0, "e4m3")
    a0 = xtidxq.T @ wau
    xtidx2q = mxq(f64(xt)[:, idx2], 0, "e4m3")
    b0 = xtidx2q.T @ wbu
    a = a0 + f64(bi)
    b = b0 + f64(bi)
    y = a - b * np.mean(a * b, axis=1, keepdims=True) / (np.mean(np.square(b), axis=1, keepdims=True) + 0.1)
    words, scales = planes(y)
    return y, words, scales

@@ -1,0 +1,245 @@
+from contextlib import ExitStack
+
+import concourse.mybir as mybir
+from concourse.masks import make_identity
+
+K, T, J, N = 1024, 2048, 512, 512
+FLOPS = 2 * 2 * K * J * N
+
+F32 = mybir.dt.float32
+BF16 = mybir.dt.bfloat16
+I32 = mybir.dt.int32
+U32 = mybir.dt.uint32
+U16 = mybir.dt.uint16
+U8 = mybir.dt.uint8
+FP8X4 = mybir.dt.float8_e4m3fn_x4
+FP4X4 = mybir.dt.float4_e2m1fn_x4
+ACT = mybir.ActivationFunctionType
+ALU = mybir.AluOpType
+
+P = 128
+PASSES = K // 512
+PIECES = (
+    ((0, 1024, 512), (1024, 2048, 512)),
+    ((0, 1024, 256), (1024, 2048, 512)),
+    ((0, 1024, 0), (1024, 2048, 0)),
+    ((0, 1024, 0), (1024, 1536, 512), (1536, 2048, 352)),
+)
+
+
+def tile_moe_expert_less_common_part_pl_kernel(
+    tc, xt, wa_words, wa_scales, wb_words, wb_scales, bi, offs, offs2, out_0, out_1, out_2
+):
+    nc = tc.nc
+    with ExitStack() as ctx:
+        keep = ctx.enter_context(tc.tile_pool(name="keep", bufs=1))
+        psum = ctx.enter_context(tc.psum_pool(name="psum", bufs=1))
+
+        def bank(tag, name):
+            return psum.tile([P, 512], F32, name=name, tag=tag)
+
+        x_rows = xt.rearrange("(g p u e) t -> g u p e t", g=PASSES, p=P, u=2, e=2)
+        raw = {}
+        lists = []
+        wa_codes, wb_codes = [], []
+
+        def load_wa(g):
+            wa = keep.tile([P, 2 * N], U8, name=f"wa{g}", align_bytes=64)
+            nc.sync.dma_start(out=wa[:].bitcast(I32), in_=wa_words[g].bitcast(I32))
+            wa_codes.append(wa)
+
+        def load_wb(g):
+            wb = keep.tile([P, N], I32, name=f"wb{g}", align_bytes=64)
+            nc.sync.dma_start(out=wb[:], in_=wb_words[g].rearrange("p n t -> p (n t)").bitcast(I32))
+            wb_codes.append(wb)
+
+        for pair in range(4):
+            for i, (c0, c1, v) in enumerate(PIECES[pair]):
+                if pair == 3 and i == 1:
+                    load_wa(0)
+                piece = keep.tile([P, 2, c1 - c0], F32, name=f"raw{pair}_{i}")
+                nc.sync.dma_start(out=piece[:], in_=x_rows[pair // 2, pair % 2, :, :, c0:c1])
+                raw[pair, i] = piece
+                if pair == 0 and i == 0:
+                    for name, src in (("list_a", offs), ("list_b", offs2)):
+                        lst = keep.tile([P, J // 16], U16, name=name)
+                        nc.sync.dma_start(lst[:], src)
+                        lists.append(lst)
+                    bias_four = keep.tile([P, 4], F32, name="bias_four")
+                    nc.sync.dma_start(out=bias_four[:], in_=bi.rearrange("o (p c) -> (o p) c", c=4))
+        load_wb(0)
+        load_wa(1)
+        load_wb(1)
+
+        ident = keep.tile([P, P], F32, name="ident")
+        make_identity(nc, ident[:])
+        w_scales = []
+        for name, src in (("wa_sc", wa_scales), ("wb_sc", wb_scales)):
+            plane = keep.tile([P, PASSES, N], U8, name=name, align_bytes=64)
+            nc.gpsimd.memset(plane[:].rearrange("p g n -> p (g n)").bitcast(I32), 0)
+            for q in range(4):
+                nc.gpsimd.dma_start(
+                    out=plane[32 * q : 32 * q + 4].bitcast(I32),
+                    in_=src[:, 4 * q : 4 * q + 4, :].rearrange("g r n -> r g n").bitcast(I32),
+                )
+            w_scales.append(plane)
+
+        spread_ps = bank("a0", "spread_ps")
+        for c in range(4):
+            nc.tensor.transpose(
+                spread_ps[:, c * P : (c + 1) * P], bias_four[:, c : c + 1].to_broadcast([P, P]), ident[:]
+            )
+        bias_all = keep.tile([P, N], F32, name="bias_all")
+        nc.vector.tensor_copy(
+            out=bias_all[:].rearrange("p (m c) -> p m c", c=4), in_=spread_ps[:].rearrange("p (c m) -> p m c", c=4)
+        )
+        bias_ps = bank("a1", "bias_ps")
+        for nb in range(4):
+            nc.tensor.transpose(bias_ps[:, nb * P : (nb + 1) * P], bias_all[:, nb * P : (nb + 1) * P], ident[:])
+        bias_col = keep.tile([P, 4], F32, name="bias_col")
+        nc.vector.tensor_copy(out=bias_col[:], in_=bias_ps[:, 0:N:P])
+
+        a_turned = [bank(f"a{nb}", f"a_turned{nb}") for nb in range(4)]
+        b_sums = [bank(f"b{t}", f"b_sums{t}") for t in range(4)]
+
+        def cast_pair(pair):
+            window = keep.tile([P, T, 2], BF16, name=f"window{pair}")
+            for i, (c0, c1, v) in enumerate(PIECES[pair]):
+                src = raw[pair, i][:].rearrange("p e t -> p t e")
+                if v:
+                    nc.vector.tensor_copy(out=window[:, c0 : c0 + v, :], in_=src[:, 0:v, :])
+                if v < c1 - c0:
+                    nc.scalar.activation(out=window[:, c0 + v : c1, :], in_=src[:, v:, :], func=ACT.Copy)
+            return window[:].rearrange("p t e -> p (t e)").bitcast(U32)
+
+        for g in range(PASSES):
+            picked = [keep.tile([P, 2, J], U32, name=f"picked{g}_{s}") for s in range(2)]
+            for u in range(2):
+                words = cast_pair(2 * g + u)
+                for s in range(2):
+                    nc.vector.tensor_copy(out=picked[s][:, u, :], in_=words.indirect(lists[s][:]))
+            codes, scales = [], []
+            for s in range(2):
+                woven = keep.tile([P, 4 * J], BF16, name=f"woven{g}_{s}", align_bytes=64)
+                dst = woven[:].bitcast(U32).rearrange("p (t m u) -> p m u t", t=4, u=2)
+                src = picked[s][:].rearrange("p u (m t) -> p m u t", t=4)
+                if g == 0:
+                    nc.vector.tensor_copy(out=dst.bitcast(I32), in_=src.bitcast(I32))
+                else:
+                    nc.scalar.copy(out=dst, in_=src)
+                cd = keep.tile([P, J], U32, name=f"codes{g}_{s}", align_bytes=64)
+                sc = keep.tile([P, J], U8, name=f"scales{g}_{s}", align_bytes=64)
+                nc.vector.quantize_mx(out=cd[:].bitcast(FP8X4), scales=sc[:], in_=woven[:])
+                codes.append(cd)
+                scales.append(sc)
+            for nb in range(4):
+                nc.tensor.matmul_mx(
+                    out=a_turned[nb][:],
+                    lhsT=wa_codes[g][:, 2 * P * nb : 2 * P * (nb + 1)].bitcast(FP4X4),
+                    lhsT_scale=w_scales[0][:, g, P * nb : P * (nb + 1)],
+                    rhs=codes[0][:].bitcast(FP8X4),
+                    rhs_scale=scales[0][:],
+                    start=(g == 0),
+                    stop=(g == PASSES - 1),
+                )
+            for t in range(4):
+                nc.tensor.matmul_mx(
+                    out=b_sums[t][:],
+                    lhsT=codes[1][:, P * t : P * (t + 1)].bitcast(FP8X4),
+                    lhsT_scale=scales[1][:, P * t : P * (t + 1)],
+                    rhs=wb_codes[g][:].bitcast(FP8X4),
+                    rhs_scale=w_scales[1][:, g, :],
+                    start=(g == 0),
+                    stop=(g == PASSES - 1),
+                )
+
+        a_cols = []
+        for nb in range(4):
+            ac = keep.tile([P, J], F32, name=f"a_cols{nb}")
+            if nb == 1:
+                nc.vector.tensor_scalar(
+                    out=ac[:], in0=a_turned[nb][:], scalar1=bias_col[:, nb : nb + 1], scalar2=None, op0=ALU.add
+                )
+            else:
+                nc.scalar.activation(
+                    out=ac[:], in_=a_turned[nb][:], func=ACT.Identity, bias=bias_col[:, nb : nb + 1], scale=1.0
+                )
+            a_cols.append(ac)
+        a_rows = []
+        for t in range(4):
+            ar = bank(f"a{t}", f"a_rows{t}")
+            for nb in range(4):
+                nc.tensor.transpose(ar[:, P * nb : P * (nb + 1)], a_cols[nb][:, P * t : P * (t + 1)], ident[:])
+            a_rows.append(ar)
+
+        b_rows, sq = [], []
+        for t in range(4):
+            br = keep.tile([P, N], F32, name=f"b_rows{t}")
+            nc.vector.tensor_tensor(out=br[:], in0=b_sums[t][:], in1=bias_all[:], op=ALU.add)
+            b_rows.append(br)
+        squares = keep.tile([P, N], F32, name="squares")
+        for h in range(2):
+            s = keep.tile([P, 2], F32, name=f"sq{h}")
+            for i in range(2):
+                nc.scalar.activation(
+                    out=squares[:], in_=b_rows[2 * h + i][:], func=ACT.Square, accum_out=s[:, i : i + 1]
+                )
+            sq.append(s)
+
+        y = [keep.tile([P, 2, N], F32, name=f"y{h}") for h in range(2)]
+        y_hbm = out_0.rearrange("(p t) n -> p t n", t=4)
+        products = keep.tile([P, N], F32, name="products")
+        rounded = keep.tile([P, N, 4], BF16, name="rounded", align_bytes=64)
+        inv = []
+        share = [keep.tile([P, 1], F32, name=f"share{t}") for t in range(4)]
+
+        def inverse(h):
+            den = keep.tile([P, 2], F32, name=f"den{h}")
+            nc.vector.tensor_scalar(
+                out=den[:], in0=sq[h][:], scalar1=0.1 * N, scalar2=-1.0, op0=ALU.add, op1=ALU.mult
+            )
+            r = keep.tile([P, 2], F32, name=f"inv{h}")
+            nc.vector.reciprocal(out=r[:], in_=den[:])
+            inv.append(r)
+
+        def common(t):
+            nc.vector.scalar_tensor_tensor(
+                out=products[:], in0=a_rows[t][:], scalar=inv[t // 2][:, t % 2 : t % 2 + 1], in1=b_rows[t][:],
+                op0=ALU.mult, op1=ALU.mult, accum_out=share[t][:],
+            )
+
+        def finish(t):
+            nc.vector.scalar_tensor_tensor(
+                out=y[t // 2][:, t % 2, :], in0=b_rows[t][:], scalar=share[t][:], in1=a_rows[t][:],
+                op0=ALU.mult, op1=ALU.add,
+            )
+            nc.sync.dma_start(out=y_hbm[:, t, :], in_=y[t // 2][:, t % 2, :])
+
+        inverse(0)
+        common(0)
+        common(1)
+        finish(0)
+        inverse(1)
+        finish(1)
+        nc.scalar.activation(out=rounded[:, :, 0:2], in_=y[0][:].rearrange("p e n -> p n e"), func=ACT.Copy)
+        common(2)
+        common(3)
+        finish(2)
+        finish(3)
+        split = 320
+        last = y[1][:].rearrange("p e n -> p n e")
+        nc.vector.tensor_copy(out=rounded[:, 0:split, 2:4], in_=last[:, 0:split, :])
+        nc.scalar.activation(out=rounded[:, split:N, 2:4], in_=last[:, split:N, :], func=ACT.Copy)
+        y_codes = keep.tile([P, N], U32, name="y_codes", align_bytes=64)
+        y_scales = keep.tile([P, N], U8, name="y_scales", align_bytes=64)
+        nc.vector.quantize_mx(
+            out=y_codes[:].bitcast(FP8X4), scales=y_scales[:], in_=rounded[:].rearrange("p n t -> p (n t)")
+        )
+        nc.sync.dma_start(
+            out=out_1[0].rearrange("p n t -> p (n t)").bitcast(I32), in_=y_codes[:].bitcast(I32)
+        )
+        for q in range(4):
+            queue = nc.scalar if q % 2 else nc.sync
+            queue.dma_start(
+                out=out_2[0, 4 * q : 4 * q + 4, :].bitcast(I32), in_=y_scales[32 * q : 32 * q + 4, :].bitcast(I32)
+            )

@@ -20,9 +20,9 @@ ALU = mybir.AluOpType
 P = 128
 PASSES = K // 512
 PIECES = (
-    ((0, 1024, 512), (1024, 2048, 512)),
-    ((0, 1024, 256), (1024, 2048, 512)),
-    ((0, 1024, 0), (1024, 2048, 0)),
+    ((0, 2048, 1344),),
+    ((0, 1024, 0), (1024, 2048, 640)),
+    ((0, 512, 0), (512, 1024, 0), (1024, 2048, 512)),
     ((0, 1024, 0), (1024, 1536, 512), (1536, 2048, 352)),
 )
 
@@ -39,6 +39,19 @@ def tile_moe_expert_less_common_part_pl_kernel(
             return psum.tile([P, 512], F32, name=name, tag=tag)
 
         x_rows = xt.rearrange("(g p u e) t -> g u p e t", g=PASSES, p=P, u=2, e=2)
+        w_scales = []
+        for name in ("wa_sc", "wb_sc"):
+            plane = keep.tile([P, PASSES, N], U8, name=name, align_bytes=64)
+            nc.vector.memset(plane[:].rearrange("p g n -> p (g n)").bitcast(I32), 0)
+            w_scales.append(plane)
+
+        def load_scales(plane, src):
+            for q in range(4):
+                nc.sync.dma_start(
+                    out=plane[32 * q : 32 * q + 4].bitcast(I32),
+                    in_=src[:, 4 * q : 4 * q + 4, :].rearrange("g r n -> r g n").bitcast(I32),
+                )
+
         raw = {}
         lists = []
         wa_codes, wb_codes = [], []
@@ -55,9 +68,7 @@ def tile_moe_expert_less_common_part_pl_kernel(
 
         for pair in range(4):
             for i, (c0, c1, v) in enumerate(PIECES[pair]):
-                if pair == 3 and i == 1:
-                    load_wa(0)
-                piece = keep.tile([P, 2, c1 - c0], F32, name=f"raw{pair}_{i}")
+                piece = keep.tile([P, 2, c1 - c0], F32, name=f"raw{pair}_{i}", align_bytes=64)
                 nc.sync.dma_start(out=piece[:], in_=x_rows[pair // 2, pair % 2, :, :, c0:c1])
                 raw[pair, i] = piece
                 if pair == 0 and i == 0:
@@ -67,22 +78,15 @@ def tile_moe_expert_less_common_part_pl_kernel(
                         lists.append(lst)
                     bias_four = keep.tile([P, 4], F32, name="bias_four")
                     nc.sync.dma_start(out=bias_four[:], in_=bi.rearrange("o (p c) -> (o p) c", c=4))
+        load_scales(w_scales[0], wa_scales)
+        load_wa(0)
+        load_scales(w_scales[1], wb_scales)
         load_wb(0)
         load_wa(1)
         load_wb(1)
 
         ident = keep.tile([P, P], F32, name="ident")
         make_identity(nc, ident[:])
-        w_scales = []
-        for name, src in (("wa_sc", wa_scales), ("wb_sc", wb_scales)):
-            plane = keep.tile([P, PASSES, N], U8, name=name, align_bytes=64)
-            nc.gpsimd.memset(plane[:].rearrange("p g n -> p (g n)").bitcast(I32), 0)
-            for q in range(4):
-                nc.gpsimd.dma_start(
-                    out=plane[32 * q : 32 * q + 4].bitcast(I32),
-                    in_=src[:, 4 * q : 4 * q + 4, :].rearrange("g r n -> r g n").bitcast(I32),
-                )
-            w_scales.append(plane)
 
         spread_ps = bank("a0", "spread_ps")
         for c in range(4):
@@ -96,148 +100,203 @@ def tile_moe_expert_less_common_part_pl_kernel(
         bias_ps = bank("a1", "bias_ps")
         for nb in range(4):
             nc.tensor.transpose(bias_ps[:, nb * P : (nb + 1) * P], bias_all[:, nb * P : (nb + 1) * P], ident[:])
-        bias_col = keep.tile([P, 4], F32, name="bias_col")
-        nc.vector.tensor_copy(out=bias_col[:], in_=bias_ps[:, 0:N:P])
+        neg_bias_col = keep.tile([P, 4], F32, name="neg_bias_col")
+        nc.vector.tensor_scalar(
+            out=neg_bias_col[:], in0=bias_ps[:, 0:N:P], scalar1=-1.0, scalar2=None, op0=ALU.mult
+        )
 
         a_turned = [bank(f"a{nb}", f"a_turned{nb}") for nb in range(4)]
         b_sums = [bank(f"b{t}", f"b_sums{t}") for t in range(4)]
+        cuts = ((0, J), (0, J // 2, J))
+        picked = {
+            (g, s, j0): keep.tile([P, 2, j1 - j0], U32, name=f"picked{g}_{s}_{j0}")
+            for g in range(PASSES)
+            for s in range(2)
+            for j0, j1 in zip(cuts[g], cuts[g][1:])
+        }
+        woven = {}
+        codes = [
+            [keep.tile([P, J], U32, name=f"codes{g}_{s}", align_bytes=64) for s in range(2)] for g in range(PASSES)
+        ]
+        scales = [
+            [keep.tile([P, J], U8, name=f"scales{g}_{s}", align_bytes=64) for s in range(2)] for g in range(PASSES)
+        ]
+        windows = [keep.tile([P, T, 2], BF16, name=f"window{pair}") for pair in range(4)]
 
-        def cast_pair(pair):
-            window = keep.tile([P, T, 2], BF16, name=f"window{pair}")
-            for i, (c0, c1, v) in enumerate(PIECES[pair]):
-                src = raw[pair, i][:].rearrange("p e t -> p t e")
-                if v:
-                    nc.vector.tensor_copy(out=window[:, c0 : c0 + v, :], in_=src[:, 0:v, :])
-                if v < c1 - c0:
-                    nc.scalar.activation(out=window[:, c0 + v : c1, :], in_=src[:, v:, :], func=ACT.Copy)
-            return window[:].rearrange("p t e -> p (t e)").bitcast(U32)
+        def cast(pair, i):
+            c0, c1, v = PIECES[pair][i]
+            src = raw[pair, i][:].rearrange("p e t -> p t e")
+            if v:
+                nc.vector.tensor_copy(out=windows[pair][:, c0 : c0 + v, :], in_=src[:, 0:v, :])
+            if v < c1 - c0:
+                nc.scalar.activation(out=windows[pair][:, c0 + v : c1, :], in_=src[:, v:, :], func=ACT.Copy)
 
-        for g in range(PASSES):
-            picked = [keep.tile([P, 2, J], U32, name=f"picked{g}_{s}") for s in range(2)]
-            for u in range(2):
-                words = cast_pair(2 * g + u)
-                for s in range(2):
-                    nc.vector.tensor_copy(out=picked[s][:, u, :], in_=words.indirect(lists[s][:]))
-            codes, scales = [], []
-            for s in range(2):
-                woven = keep.tile([P, 4 * J], BF16, name=f"woven{g}_{s}", align_bytes=64)
-                dst = woven[:].bitcast(U32).rearrange("p (t m u) -> p m u t", t=4, u=2)
-                src = picked[s][:].rearrange("p u (m t) -> p m u t", t=4)
-                if g == 0:
-                    nc.vector.tensor_copy(out=dst.bitcast(I32), in_=src.bitcast(I32))
-                else:
-                    nc.scalar.copy(out=dst, in_=src)
-                cd = keep.tile([P, J], U32, name=f"codes{g}_{s}", align_bytes=64)
-                sc = keep.tile([P, J], U8, name=f"scales{g}_{s}", align_bytes=64)
-                nc.vector.quantize_mx(out=cd[:].bitcast(FP8X4), scales=sc[:], in_=woven[:])
-                codes.append(cd)
-                scales.append(sc)
-            for nb in range(4):
+        def gather(pair, s, j0, j1):
+            words = windows[pair][:].rearrange("p t e -> p (t e)").bitcast(U32)
+            entries = lists[s][:, j0 // 16 : j1 // 16]
+            nc.vector.tensor_copy(out=picked[pair // 2, s, j0][:, pair % 2, :], in_=words.indirect(entries))
+
+        def weave_views(g, s, j0, j1):
+            dst = woven[g, s][:].bitcast(U32).rearrange("p (t m u) -> p m u t", t=4, u=2)
+            src = picked[g, s, j0][:].rearrange("p u (m t) -> p m u t", t=4)
+            return dst[:, j0 // 4 : j1 // 4], src
+
+        def quantise(g, s):
+            nc.vector.quantize_mx(out=codes[g][s][:].bitcast(FP8X4), scales=scales[g][s][:], in_=woven[g, s][:])
+
+        def multiply_a(g, blocks):
+            for nb in blocks:
                 nc.tensor.matmul_mx(
                     out=a_turned[nb][:],
                     lhsT=wa_codes[g][:, 2 * P * nb : 2 * P * (nb + 1)].bitcast(FP4X4),
                     lhsT_scale=w_scales[0][:, g, P * nb : P * (nb + 1)],
-                    rhs=codes[0][:].bitcast(FP8X4),
-                    rhs_scale=scales[0][:],
+                    rhs=codes[g][0][:].bitcast(FP8X4),
+                    rhs_scale=scales[g][0][:],
                     start=(g == 0),
                     stop=(g == PASSES - 1),
                 )
-            for t in range(4):
+
+        def multiply_b(g, blocks):
+            for t in blocks:
                 nc.tensor.matmul_mx(
                     out=b_sums[t][:],
-                    lhsT=codes[1][:, P * t : P * (t + 1)].bitcast(FP8X4),
-                    lhsT_scale=scales[1][:, P * t : P * (t + 1)],
+                    lhsT=codes[g][1][:, P * t : P * (t + 1)].bitcast(FP8X4),
+                    lhsT_scale=scales[g][1][:, P * t : P * (t + 1)],
                     rhs=wb_codes[g][:].bitcast(FP8X4),
                     rhs_scale=w_scales[1][:, g, :],
                     start=(g == 0),
                     stop=(g == PASSES - 1),
                 )
 
-        a_cols = []
+        halves = [(s, j0, j0 + J // 2) for s in range(2) for j0 in (0, J // 2)]
+        for pair in range(2):
+            for i in range(len(PIECES[pair])):
+                cast(pair, i)
+            gather(pair, 0, 0, J)
+            gather(pair, 1, 0, J)
+        cast(2, 0)
+        cast(2, 1)
+        woven[0, 0] = keep.tile([P, 4 * J], BF16, name="woven0_0", tag="raw2_1", align_bytes=64)
+        for g, s in ((0, 1), (1, 0), (1, 1)):
+            woven[g, s] = keep.tile([P, 4 * J], BF16, name=f"woven{g}_{s}", align_bytes=64)
+        dst, src = weave_views(0, 0, 0, J)
+        nc.scalar.copy(out=dst, in_=src)
+        dst, src = weave_views(0, 1, 0, J)
+        nc.vector.tensor_copy(out=dst.bitcast(I32), in_=src.bitcast(I32))
+        quantise(0, 1)
+        cast(2, 2)
+        quantise(0, 0)
+        for half in halves:
+            gather(2, *half)
+        multiply_a(0, range(4))
+        multiply_b(0, range(4))
+        for i in range(len(PIECES[3])):
+            cast(3, i)
+        for half in halves:
+            gather(3, *half)
+            dst, src = weave_views(1, *half)
+            nc.scalar.copy(out=dst, in_=src)
+        quantise(1, 0)
+        quantise(1, 1)
+        multiply_a(1, range(3))
+        multiply_b(1, range(1))
+        multiply_a(1, range(3, 4))
+        multiply_b(1, range(1, 4))
+
+        neg_a_cols = []
         for nb in range(4):
-            ac = keep.tile([P, J], F32, name=f"a_cols{nb}")
-            if nb == 1:
+            ac = keep.tile([P, J], F32, name=f"neg_a_cols{nb}")
+            col = neg_bias_col[:, nb : nb + 1]
+            if nb == 0:
                 nc.vector.tensor_scalar(
-                    out=ac[:], in0=a_turned[nb][:], scalar1=bias_col[:, nb : nb + 1], scalar2=None, op0=ALU.add
+                    out=ac[:], in0=a_turned[nb][:], scalar1=-1.0, scalar2=col, op0=ALU.mult, op1=ALU.add
                 )
             else:
-                nc.scalar.activation(
-                    out=ac[:], in_=a_turned[nb][:], func=ACT.Identity, bias=bias_col[:, nb : nb + 1], scale=1.0
-                )
-            a_cols.append(ac)
-        a_rows = []
+                nc.scalar.activation(out=ac[:], in_=a_turned[nb][:], func=ACT.Identity, bias=col, scale=-1.0)
+            neg_a_cols.append(ac)
+        neg_a = []
         for t in range(4):
-            ar = bank(f"a{t}", f"a_rows{t}")
+            ar = bank(f"a{t}", f"neg_a{t}")
             for nb in range(4):
-                nc.tensor.transpose(ar[:, P * nb : P * (nb + 1)], a_cols[nb][:, P * t : P * (t + 1)], ident[:])
-            a_rows.append(ar)
+                nc.tensor.transpose(ar[:, P * nb : P * (nb + 1)], neg_a_cols[nb][:, P * t : P * (t + 1)], ident[:])
+            neg_a.append(ar)
 
-        b_rows, sq = [], []
-        for t in range(4):
-            br = keep.tile([P, N], F32, name=f"b_rows{t}")
-            nc.vector.tensor_tensor(out=br[:], in0=b_sums[t][:], in1=bias_all[:], op=ALU.add)
-            b_rows.append(br)
+        b_rows = [keep.tile([P, N], F32, name=f"b_rows{t}") for t in range(4)]
         squares = keep.tile([P, N], F32, name="squares")
-        for h in range(2):
-            s = keep.tile([P, 2], F32, name=f"sq{h}")
-            for i in range(2):
-                nc.scalar.activation(
-                    out=squares[:], in_=b_rows[2 * h + i][:], func=ACT.Square, accum_out=s[:, i : i + 1]
-                )
-            sq.append(s)
-
+        products = keep.tile([P, N], F32, name="products")
+        groups = ((0,), (1,), (2, 3))
+        sums = [keep.tile([P, len(ts)], F32, name=f"sums{h}") for h, ts in enumerate(groups)]
+        den = [keep.tile([P, len(ts)], F32, name=f"den{h}") for h, ts in enumerate(groups)]
+        inv = [keep.tile([P, len(ts)], F32, name=f"inv{h}") for h, ts in enumerate(groups)]
+        place = {t: (h, i) for h, ts in enumerate(groups) for i, t in enumerate(ts)}
+        neg_share = [keep.tile([P, 1], F32, name=f"neg_share{t}") for t in range(4)]
         y = [keep.tile([P, 2, N], F32, name=f"y{h}") for h in range(2)]
         y_hbm = out_0.rearrange("(p t) n -> p t n", t=4)
-        products = keep.tile([P, N], F32, name="products")
         rounded = keep.tile([P, N, 4], BF16, name="rounded", align_bytes=64)
-        inv = []
-        share = [keep.tile([P, 1], F32, name=f"share{t}") for t in range(4)]
+        y_codes = keep.tile([P, N], U32, name="y_codes", align_bytes=64)
+        y_scales = keep.tile([P, N], U8, name="y_scales", align_bytes=64)
+        words_hbm = out_1[0].rearrange("p n t -> p (n t)").bitcast(I32)
 
-        def inverse(h):
-            den = keep.tile([P, 2], F32, name=f"den{h}")
-            nc.vector.tensor_scalar(
-                out=den[:], in0=sq[h][:], scalar1=0.1 * N, scalar2=-1.0, op0=ALU.add, op1=ALU.mult
-            )
-            r = keep.tile([P, 2], F32, name=f"inv{h}")
-            nc.vector.reciprocal(out=r[:], in_=den[:])
-            inv.append(r)
+        def make_b(t):
+            h, i = place[t]
+            nc.vector.tensor_tensor(out=b_rows[t][:], in0=b_sums[t][:], in1=bias_all[:], op=ALU.add)
+            nc.scalar.activation(out=squares[:], in_=b_rows[t][:], func=ACT.Square, accum_out=sums[h][:, i : i + 1])
+            if t == groups[h][-1]:
+                nc.scalar.activation(out=den[h][:], in_=sums[h][:], func=ACT.Copy, bias=0.1 * N, scale=1.0)
+
+        def invert(h):
+            nc.vector.reciprocal(out=inv[h][:], in_=den[h][:])
 
         def common(t):
+            h, i = place[t]
             nc.vector.scalar_tensor_tensor(
-                out=products[:], in0=a_rows[t][:], scalar=inv[t // 2][:, t % 2 : t % 2 + 1], in1=b_rows[t][:],
-                op0=ALU.mult, op1=ALU.mult, accum_out=share[t][:],
+                out=products[:], in0=neg_a[t][:], scalar=inv[h][:, i : i + 1], in1=b_rows[t][:],
+                op0=ALU.mult, op1=ALU.mult, accum_out=neg_share[t][:],
             )
 
-        def finish(t):
+        def finish(t, cols):
             nc.vector.scalar_tensor_tensor(
-                out=y[t // 2][:, t % 2, :], in0=b_rows[t][:], scalar=share[t][:], in1=a_rows[t][:],
-                op0=ALU.mult, op1=ALU.add,
+                out=y[t // 2][:, t % 2, cols], in0=b_rows[t][:, cols], scalar=neg_share[t][:], in1=neg_a[t][:, cols],
+                op0=ALU.mult, op1=ALU.subtract,
             )
+
+        def store(t):
             nc.sync.dma_start(out=y_hbm[:, t, :], in_=y[t // 2][:, t % 2, :])
 
-        inverse(0)
+        def planes(cols):
+            nc.vector.quantize_mx(
+                out=y_codes[:, cols].bitcast(FP8X4),
+                scales=y_scales[:, cols],
+                in_=rounded[:, cols, :].rearrange("p n t -> p (n t)"),
+            )
+            nc.sync.dma_start(out=words_hbm[:, cols], in_=y_codes[:, cols].bitcast(I32))
+
+        whole, left, right = slice(0, N), slice(0, N // 2), slice(N // 2, N)
+        for t in range(3):
+            make_b(t)
+        invert(0)
+        make_b(3)
+        invert(1)
         common(0)
         common(1)
-        finish(0)
-        inverse(1)
-        finish(1)
+        finish(0, whole)
+        store(0)
+        invert(2)
+        finish(1, whole)
+        store(1)
         nc.scalar.activation(out=rounded[:, :, 0:2], in_=y[0][:].rearrange("p e n -> p n e"), func=ACT.Copy)
         common(2)
         common(3)
-        finish(2)
-        finish(3)
-        split = 320
+        finish(2, whole)
+        store(2)
+        finish(3, left)
+        finish(3, right)
+        store(3)
         last = y[1][:].rearrange("p e n -> p n e")
-        nc.vector.tensor_copy(out=rounded[:, 0:split, 2:4], in_=last[:, 0:split, :])
-        nc.scalar.activation(out=rounded[:, split:N, 2:4], in_=last[:, split:N, :], func=ACT.Copy)
-        y_codes = keep.tile([P, N], U32, name="y_codes", align_bytes=64)
-        y_scales = keep.tile([P, N], U8, name="y_scales", align_bytes=64)
-        nc.vector.quantize_mx(
-            out=y_codes[:].bitcast(FP8X4), scales=y_scales[:], in_=rounded[:].rearrange("p n t -> p (n t)")
-        )
-        nc.sync.dma_start(
-            out=out_1[0].rearrange("p n t -> p (n t)").bitcast(I32), in_=y_codes[:].bitcast(I32)
-        )
+        nc.scalar.activation(out=rounded[:, left, 2:4], in_=last[:, left, :], func=ACT.Copy)
+        nc.vector.tensor_copy(out=rounded[:, right, 2:4], in_=last[:, right, :])
+        planes(left)
+        planes(right)
         for q in range(4):
             queue = nc.scalar if q % 2 else nc.sync
             queue.dma_start(

@@ -18,13 +18,23 @@ ACT = mybir.ActivationFunctionType
 ALU = mybir.AluOpType
 
 P = 128
-PASSES = K // 512
-PIECES = (
-    ((0, 2048, 1344),),
-    ((0, 1024, 0), (1024, 2048, 640)),
-    ((0, 512, 0), (512, 1024, 0), (1024, 2048, 512)),
-    ((0, 1024, 0), (1024, 1536, 512), (1536, 2048, 352)),
+PACK = 4
+PASSES = K // (P * PACK)
+A, B = 0, 1
+BANK = 512
+
+
+def two_thirds(tokens):
+    return 2 * tokens // 3 // 32 * 32
+
+
+LOADS = (
+    ((T, two_thirds(T)),),
+    ((T // 2, 0), (T // 2, two_thirds(T // 2))),
+    ((T // 4, 0), (T // 4, 0), (T // 2, T // 4)),
+    ((T // 2, 0), (T // 4, T // 4), (T // 4, two_thirds(T // 4))),
 )
+GROUPS = ((0,), (1,), (2, 3))
 
 
 def tile_moe_expert_less_common_part_pl_kernel(
@@ -36,269 +46,263 @@ def tile_moe_expert_less_common_part_pl_kernel(
         psum = ctx.enter_context(tc.psum_pool(name="psum", bufs=1))
 
         def bank(tag, name):
-            return psum.tile([P, 512], F32, name=name, tag=tag)
+            return psum.tile([P, BANK], F32, name=name, tag=tag)
 
-        x_rows = xt.rearrange("(g p u e) t -> g u p e t", g=PASSES, p=P, u=2, e=2)
-        w_scales = []
-        for name in ("wa_sc", "wb_sc"):
-            plane = keep.tile([P, PASSES, N], U8, name=name, align_bytes=64)
-            nc.vector.memset(plane[:].rearrange("p g n -> p (g n)").bitcast(I32), 0)
-            w_scales.append(plane)
+        bias_four = keep.tile([P, PACK], F32, name="bias_four")
+        nc.scalar.dma_start(out=bias_four[:], in_=bi.rearrange("o (p c) -> (o p) c", c=PACK))
 
-        def load_scales(plane, src):
-            for q in range(4):
+        x_pairs = xt.rearrange("(g p u e) t -> g u p e t", g=PASSES, p=P, u=2, e=2)
+        raw, lists = {}, []
+        for pair, loads in enumerate(LOADS):
+            first = 0
+            for i, (tokens, on_vector) in enumerate(loads):
+                piece = keep.tile([P, 2, tokens], F32, name=f"raw{pair}_{i}", align_bytes=64)
+                nc.sync.dma_start(out=piece[:], in_=x_pairs[pair // 2, pair % 2, :, :, first : first + tokens])
+                raw[pair, i] = (piece, first, tokens, on_vector)
+                first = first + tokens
+            if pair == 0:
+                for name, source in (("list_a", offs), ("list_b", offs2)):
+                    entries = keep.tile([P, J // 16], U16, name=name)
+                    nc.sync.dma_start(entries[:], source)
+                    lists.append(entries)
+
+        def load_scales(name, source):
+            tile = keep.tile([P, PASSES, N], U8, name=name, align_bytes=64)
+            nc.vector.memset(tile[:].rearrange("p g n -> p (g n)").bitcast(I32), 0)
+            for q in range(PACK):
                 nc.sync.dma_start(
-                    out=plane[32 * q : 32 * q + 4].bitcast(I32),
-                    in_=src[:, 4 * q : 4 * q + 4, :].rearrange("g r n -> r g n").bitcast(I32),
+                    out=tile[32 * q : 32 * q + 4].bitcast(I32),
+                    in_=source[:, 4 * q : 4 * q + 4, :].rearrange("g r n -> r g n").bitcast(I32),
                 )
-
-        raw = {}
-        lists = []
-        wa_codes, wb_codes = [], []
+            return tile
 
         def load_wa(g):
-            wa = keep.tile([P, 2 * N], U8, name=f"wa{g}", align_bytes=64)
-            nc.sync.dma_start(out=wa[:].bitcast(I32), in_=wa_words[g].bitcast(I32))
-            wa_codes.append(wa)
+            tile = keep.tile([P, 2 * N], U8, name=f"wa{g}", align_bytes=64)
+            nc.sync.dma_start(out=tile[:].bitcast(I32), in_=wa_words[g].bitcast(I32))
+            return tile
 
         def load_wb(g):
-            wb = keep.tile([P, N], I32, name=f"wb{g}", align_bytes=64)
-            nc.sync.dma_start(out=wb[:], in_=wb_words[g].rearrange("p n t -> p (n t)").bitcast(I32))
-            wb_codes.append(wb)
+            tile = keep.tile([P, N], I32, name=f"wb{g}", align_bytes=64)
+            nc.sync.dma_start(out=tile[:], in_=wb_words[g].rearrange("p n r -> p (n r)").bitcast(I32))
+            return tile
 
-        for pair in range(4):
-            for i, (c0, c1, v) in enumerate(PIECES[pair]):
-                piece = keep.tile([P, 2, c1 - c0], F32, name=f"raw{pair}_{i}", align_bytes=64)
-                nc.sync.dma_start(out=piece[:], in_=x_rows[pair // 2, pair % 2, :, :, c0:c1])
-                raw[pair, i] = piece
-                if pair == 0 and i == 0:
-                    for name, src in (("list_a", offs), ("list_b", offs2)):
-                        lst = keep.tile([P, J // 16], U16, name=name)
-                        nc.sync.dma_start(lst[:], src)
-                        lists.append(lst)
-                    bias_four = keep.tile([P, 4], F32, name="bias_four")
-                    nc.sync.dma_start(out=bias_four[:], in_=bi.rearrange("o (p c) -> (o p) c", c=4))
-        load_scales(w_scales[0], wa_scales)
-        load_wa(0)
-        load_scales(w_scales[1], wb_scales)
-        load_wb(0)
-        load_wa(1)
-        load_wb(1)
+        wa_scale = load_scales("wa_scale", wa_scales)
+        wa = [load_wa(0)]
+        wb_scale = load_scales("wb_scale", wb_scales)
+        wb = [load_wb(0)]
+        wa.append(load_wa(1))
+        wb.append(load_wb(1))
 
         ident = keep.tile([P, P], F32, name="ident")
         make_identity(nc, ident[:])
+        minus_one = keep.tile([P, 2], F32, name="minus_one")
+        nc.gpsimd.memset(minus_one[:], -1.0)
 
-        spread_ps = bank("a0", "spread_ps")
-        for c in range(4):
-            nc.tensor.transpose(
-                spread_ps[:, c * P : (c + 1) * P], bias_four[:, c : c + 1].to_broadcast([P, P]), ident[:]
-            )
-        bias_all = keep.tile([P, N], F32, name="bias_all")
+        spread = bank("a0", "spread")
+        for c in range(PACK):
+            nc.tensor.transpose(spread[:, c * P : (c + 1) * P], bias_four[:, c : c + 1].to_broadcast([P, P]), ident[:])
+        bias_rows = keep.tile([P, N], F32, name="bias_rows")
         nc.vector.tensor_copy(
-            out=bias_all[:].rearrange("p (m c) -> p m c", c=4), in_=spread_ps[:].rearrange("p (c m) -> p m c", c=4)
+            out=bias_rows[:].rearrange("p (m c) -> p m c", c=PACK), in_=spread[:].rearrange("p (c m) -> p m c", c=PACK)
         )
-        bias_ps = bank("a1", "bias_ps")
-        for nb in range(4):
-            nc.tensor.transpose(bias_ps[:, nb * P : (nb + 1) * P], bias_all[:, nb * P : (nb + 1) * P], ident[:])
-        neg_bias_col = keep.tile([P, 4], F32, name="neg_bias_col")
-        nc.vector.tensor_scalar(
-            out=neg_bias_col[:], in0=bias_ps[:, 0:N:P], scalar1=-1.0, scalar2=None, op0=ALU.mult
-        )
+        upright = bank("a1", "upright")
+        for nb in range(PACK):
+            nc.tensor.transpose(upright[:, nb * P : (nb + 1) * P], bias_rows[:, nb * P : (nb + 1) * P], ident[:])
+        neg_bias_cols = keep.tile([P, PACK], F32, name="neg_bias_cols")
+        nc.vector.tensor_scalar(out=neg_bias_cols[:], in0=upright[:, 0:N:P], scalar1=-1.0, scalar2=None, op0=ALU.mult)
 
-        a_turned = [bank(f"a{nb}", f"a_turned{nb}") for nb in range(4)]
-        b_sums = [bank(f"b{t}", f"b_sums{t}") for t in range(4)]
-        cuts = ((0, J), (0, J // 2, J))
+        a_turned = [bank(f"a{nb}", f"a_turned{nb}") for nb in range(PACK)]
+        b_sums = [bank(f"b{t}", f"b_sums{t}") for t in range(PACK)]
+        windows = [keep.tile([P, T, 2], BF16, name=f"window{pair}") for pair in range(len(LOADS))]
+        wholes = [(s, 0, J) for s in (A, B)]
+        halves = [(s, j0, j0 + J // 2) for s in (A, B) for j0 in (0, J // 2)]
         picked = {
             (g, s, j0): keep.tile([P, 2, j1 - j0], U32, name=f"picked{g}_{s}_{j0}")
-            for g in range(PASSES)
-            for s in range(2)
-            for j0, j1 in zip(cuts[g], cuts[g][1:])
+            for g, parts in enumerate((wholes, halves))
+            for s, j0, j1 in parts
         }
         woven = {}
-        codes = [
-            [keep.tile([P, J], U32, name=f"codes{g}_{s}", align_bytes=64) for s in range(2)] for g in range(PASSES)
-        ]
-        scales = [
-            [keep.tile([P, J], U8, name=f"scales{g}_{s}", align_bytes=64) for s in range(2)] for g in range(PASSES)
-        ]
-        windows = [keep.tile([P, T, 2], BF16, name=f"window{pair}") for pair in range(4)]
+        operands = [(g, s) for g in range(PASSES) for s in (A, B)]
+        codes = {(g, s): keep.tile([P, J], U32, name=f"codes{g}_{s}", align_bytes=64) for g, s in operands}
+        scales = {(g, s): keep.tile([P, J], U8, name=f"scales{g}_{s}", align_bytes=64) for g, s in operands}
 
         def cast(pair, i):
-            c0, c1, v = PIECES[pair][i]
-            src = raw[pair, i][:].rearrange("p e t -> p t e")
-            if v:
-                nc.vector.tensor_copy(out=windows[pair][:, c0 : c0 + v, :], in_=src[:, 0:v, :])
-            if v < c1 - c0:
-                nc.scalar.activation(out=windows[pair][:, c0 + v : c1, :], in_=src[:, v:, :], func=ACT.Copy)
+            piece, first, tokens, on_vector = raw[pair, i]
+            by_token = piece[:].rearrange("p e t -> p t e")
+            target = windows[pair][:, first : first + tokens, :]
+            if on_vector > 0:
+                nc.vector.tensor_copy(out=target[:, 0:on_vector, :], in_=by_token[:, 0:on_vector, :])
+            if on_vector < tokens:
+                nc.scalar.activation(out=target[:, on_vector:, :], in_=by_token[:, on_vector:, :], func=ACT.Copy)
 
         def gather(pair, s, j0, j1):
             words = windows[pair][:].rearrange("p t e -> p (t e)").bitcast(U32)
-            entries = lists[s][:, j0 // 16 : j1 // 16]
-            nc.vector.tensor_copy(out=picked[pair // 2, s, j0][:, pair % 2, :], in_=words.indirect(entries))
+            nc.vector.tensor_copy(
+                out=picked[pair // 2, s, j0][:, pair % 2, :], in_=words.indirect(lists[s][:, j0 // 16 : j1 // 16])
+            )
 
         def weave_views(g, s, j0, j1):
-            dst = woven[g, s][:].bitcast(U32).rearrange("p (t m u) -> p m u t", t=4, u=2)
-            src = picked[g, s, j0][:].rearrange("p u (m t) -> p m u t", t=4)
-            return dst[:, j0 // 4 : j1 // 4], src
+            target = woven[g, s][:].bitcast(U32).rearrange("p (t m u) -> p m u t", t=PACK, u=2)
+            return target[:, j0 // PACK : j1 // PACK], picked[g, s, j0][:].rearrange("p u (m t) -> p m u t", t=PACK)
 
         def quantise(g, s):
-            nc.vector.quantize_mx(out=codes[g][s][:].bitcast(FP8X4), scales=scales[g][s][:], in_=woven[g, s][:])
+            nc.vector.quantize_mx(out=codes[g, s][:].bitcast(FP8X4), scales=scales[g, s][:], in_=woven[g, s][:])
 
         def multiply_a(g, blocks):
             for nb in blocks:
                 nc.tensor.matmul_mx(
                     out=a_turned[nb][:],
-                    lhsT=wa_codes[g][:, 2 * P * nb : 2 * P * (nb + 1)].bitcast(FP4X4),
-                    lhsT_scale=w_scales[0][:, g, P * nb : P * (nb + 1)],
-                    rhs=codes[g][0][:].bitcast(FP8X4),
-                    rhs_scale=scales[g][0][:],
+                    lhsT=wa[g][:, 2 * P * nb : 2 * P * (nb + 1)].bitcast(FP4X4),
+                    lhsT_scale=wa_scale[:, g, P * nb : P * (nb + 1)],
+                    rhs=codes[g, A][:].bitcast(FP8X4),
+                    rhs_scale=scales[g, A][:],
                     start=(g == 0),
                     stop=(g == PASSES - 1),
                 )
 
-        def multiply_b(g, blocks):
-            for t in blocks:
+        def multiply_b(g, tiles):
+            for t in tiles:
                 nc.tensor.matmul_mx(
                     out=b_sums[t][:],
-                    lhsT=codes[g][1][:, P * t : P * (t + 1)].bitcast(FP8X4),
-                    lhsT_scale=scales[g][1][:, P * t : P * (t + 1)],
-                    rhs=wb_codes[g][:].bitcast(FP8X4),
-                    rhs_scale=w_scales[1][:, g, :],
+                    lhsT=codes[g, B][:, P * t : P * (t + 1)].bitcast(FP8X4),
+                    lhsT_scale=scales[g, B][:, P * t : P * (t + 1)],
+                    rhs=wb[g][:].bitcast(FP8X4),
+                    rhs_scale=wb_scale[:, g, :],
                     start=(g == 0),
                     stop=(g == PASSES - 1),
                 )
 
-        halves = [(s, j0, j0 + J // 2) for s in range(2) for j0 in (0, J // 2)]
-        for pair in range(2):
-            for i in range(len(PIECES[pair])):
+        for pair in (0, 1):
+            for i in range(len(LOADS[pair])):
                 cast(pair, i)
-            gather(pair, 0, 0, J)
-            gather(pair, 1, 0, J)
+            for part in wholes:
+                gather(pair, *part)
         cast(2, 0)
         cast(2, 1)
-        woven[0, 0] = keep.tile([P, 4 * J], BF16, name="woven0_0", tag="raw2_1", align_bytes=64)
-        for g, s in ((0, 1), (1, 0), (1, 1)):
-            woven[g, s] = keep.tile([P, 4 * J], BF16, name=f"woven{g}_{s}", align_bytes=64)
-        dst, src = weave_views(0, 0, 0, J)
-        nc.scalar.copy(out=dst, in_=src)
-        dst, src = weave_views(0, 1, 0, J)
-        nc.vector.tensor_copy(out=dst.bitcast(I32), in_=src.bitcast(I32))
-        quantise(0, 1)
+        woven[0, A] = keep.tile([P, PACK * J], BF16, name="woven0_0", tag="raw2_1", align_bytes=64)
+        for g, s in operands[1:]:
+            woven[g, s] = keep.tile([P, PACK * J], BF16, name=f"woven{g}_{s}", align_bytes=64)
+        target, source = weave_views(0, *wholes[A])
+        nc.scalar.copy(out=target, in_=source)
+        target, source = weave_views(0, *wholes[B])
+        nc.vector.tensor_copy(out=target.bitcast(I32), in_=source.bitcast(I32))
+        quantise(0, B)
         cast(2, 2)
-        quantise(0, 0)
-        for half in halves:
-            gather(2, *half)
-        multiply_a(0, range(4))
-        multiply_b(0, range(4))
-        for i in range(len(PIECES[3])):
+        quantise(0, A)
+        for part in halves:
+            gather(2, *part)
+        multiply_a(0, range(PACK))
+        multiply_b(0, range(PACK))
+        for i in range(len(LOADS[3])):
             cast(3, i)
-        for half in halves:
-            gather(3, *half)
-            dst, src = weave_views(1, *half)
-            nc.scalar.copy(out=dst, in_=src)
-        quantise(1, 0)
-        quantise(1, 1)
-        multiply_a(1, range(3))
+        for part in halves:
+            gather(3, *part)
+            target, source = weave_views(1, *part)
+            nc.scalar.copy(out=target, in_=source)
+        quantise(1, A)
+        quantise(1, B)
+        multiply_a(1, range(PACK - 1))
         multiply_b(1, range(1))
-        multiply_a(1, range(3, 4))
-        multiply_b(1, range(1, 4))
+        multiply_a(1, range(PACK - 1, PACK))
+        multiply_b(1, range(1, PACK))
 
-        neg_a_cols = []
-        for nb in range(4):
-            ac = keep.tile([P, J], F32, name=f"neg_a_cols{nb}")
-            col = neg_bias_col[:, nb : nb + 1]
-            if nb == 0:
-                nc.vector.tensor_scalar(
-                    out=ac[:], in0=a_turned[nb][:], scalar1=-1.0, scalar2=col, op0=ALU.mult, op1=ALU.add
+        neg_a_cols = [keep.tile([P, J], F32, name=f"neg_a_cols{nb}") for nb in range(PACK)]
+        nc.vector.tensor_scalar(
+            out=neg_a_cols[0][:], in0=a_turned[0][:], scalar1=-1.0, scalar2=neg_bias_cols[:, 0:1],
+            op0=ALU.mult, op1=ALU.add,
+        )
+        for nb in range(1, PACK):
+            nc.scalar.activation(
+                out=neg_a_cols[nb][:], in_=a_turned[nb][:], func=ACT.Identity,
+                bias=neg_bias_cols[:, nb : nb + 1], scale=-1.0,
+            )
+        neg_a = [bank(f"a{t}", f"neg_a{t}") for t in range(PACK)]
+        for t in range(PACK):
+            for nb in range(PACK):
+                nc.tensor.transpose(
+                    neg_a[t][:, P * nb : P * (nb + 1)], neg_a_cols[nb][:, P * t : P * (t + 1)], ident[:]
                 )
-            else:
-                nc.scalar.activation(out=ac[:], in_=a_turned[nb][:], func=ACT.Identity, bias=col, scale=-1.0)
-            neg_a_cols.append(ac)
-        neg_a = []
-        for t in range(4):
-            ar = bank(f"a{t}", f"neg_a{t}")
-            for nb in range(4):
-                nc.tensor.transpose(ar[:, P * nb : P * (nb + 1)], neg_a_cols[nb][:, P * t : P * (t + 1)], ident[:])
-            neg_a.append(ar)
 
-        b_rows = [keep.tile([P, N], F32, name=f"b_rows{t}") for t in range(4)]
-        squares = keep.tile([P, N], F32, name="squares")
-        products = keep.tile([P, N], F32, name="products")
-        groups = ((0,), (1,), (2, 3))
-        sums = [keep.tile([P, len(ts)], F32, name=f"sums{h}") for h, ts in enumerate(groups)]
-        den = [keep.tile([P, len(ts)], F32, name=f"den{h}") for h, ts in enumerate(groups)]
-        inv = [keep.tile([P, len(ts)], F32, name=f"inv{h}") for h, ts in enumerate(groups)]
-        place = {t: (h, i) for h, ts in enumerate(groups) for i, t in enumerate(ts)}
-        neg_share = [keep.tile([P, 1], F32, name=f"neg_share{t}") for t in range(4)]
-        y = [keep.tile([P, 2, N], F32, name=f"y{h}") for h in range(2)]
-        y_hbm = out_0.rearrange("(p t) n -> p t n", t=4)
-        rounded = keep.tile([P, N, 4], BF16, name="rounded", align_bytes=64)
-        y_codes = keep.tile([P, N], U32, name="y_codes", align_bytes=64)
-        y_scales = keep.tile([P, N], U8, name="y_scales", align_bytes=64)
-        words_hbm = out_1[0].rearrange("p n t -> p (n t)").bitcast(I32)
+        b_rows = [keep.tile([P, N], F32, name=f"b_rows{t}") for t in range(PACK)]
+        sums = [keep.tile([P, len(group)], F32, name=f"sums{h}") for h, group in enumerate(GROUPS)]
+        denominators = [keep.tile([P, len(group)], F32, name=f"den{h}") for h, group in enumerate(GROUPS)]
+        inverses = [keep.tile([P, len(group)], F32, name=f"inv{h}") for h, group in enumerate(GROUPS)]
+        place = {t: (h, i) for h, group in enumerate(GROUPS) for i, t in enumerate(group)}
+        neg_share = [keep.tile([P, 1], F32, name=f"neg_share{t}") for t in range(PACK)]
+        y = [keep.tile([P, 2, 2, N // 2], F32, name=f"y{h}") for h in range(2)]
+        y_hbm = out_0.rearrange("(p t) (half c) -> p t half c", t=PACK, half=2)
+        rounded = keep.tile([P, 2, N // 2, PACK], BF16, name="rounded", align_bytes=64)
+        y_codes = keep.tile([P, 2, N // 2], U32, name="y_codes", align_bytes=64)
+        y_scales = keep.tile([P, 2, N // 2], U8, name="y_scales", align_bytes=64)
+        words_hbm = out_1[0].rearrange("p (half c) r -> p half (c r)", half=2).bitcast(I32)
+        both, left, right = slice(0, 2), slice(0, 1), slice(1, 2)
 
         def make_b(t):
             h, i = place[t]
-            nc.vector.tensor_tensor(out=b_rows[t][:], in0=b_sums[t][:], in1=bias_all[:], op=ALU.add)
+            nc.vector.tensor_tensor(out=b_rows[t][:], in0=b_sums[t][:], in1=bias_rows[:], op=ALU.add)
+            squares = keep.tile([P, N], F32, name=f"squares{t}")
             nc.scalar.activation(out=squares[:], in_=b_rows[t][:], func=ACT.Square, accum_out=sums[h][:, i : i + 1])
-            if t == groups[h][-1]:
-                nc.scalar.activation(out=den[h][:], in_=sums[h][:], func=ACT.Copy, bias=0.1 * N, scale=1.0)
-
-        def invert(h):
-            nc.vector.reciprocal(out=inv[h][:], in_=den[h][:])
+            if t == GROUPS[h][-1]:
+                nc.scalar.activation(out=denominators[h][:], in_=sums[h][:], func=ACT.Copy, bias=0.1 * N, scale=1.0)
+                nc.gpsimd.tensor_tensor(
+                    out=inverses[h][:], in0=denominators[h][:], in1=minus_one[:, 0 : i + 1], op=ALU.pow
+                )
 
         def common(t):
             h, i = place[t]
+            products = keep.tile([P, N], F32, name=f"products{t}")
             nc.vector.scalar_tensor_tensor(
-                out=products[:], in0=neg_a[t][:], scalar=inv[h][:, i : i + 1], in1=b_rows[t][:],
+                out=products[:], in0=neg_a[t][:], scalar=inverses[h][:, i : i + 1], in1=b_rows[t][:],
                 op0=ALU.mult, op1=ALU.mult, accum_out=neg_share[t][:],
             )
 
-        def finish(t, cols):
+        def finish(t, half):
             nc.vector.scalar_tensor_tensor(
-                out=y[t // 2][:, t % 2, cols], in0=b_rows[t][:, cols], scalar=neg_share[t][:], in1=neg_a[t][:, cols],
+                out=y[t // 2][:, half, t % 2, :],
+                in0=b_rows[t][:].rearrange("p (half c) -> p half c", half=2)[:, half],
+                scalar=neg_share[t][:],
+                in1=neg_a[t][:].rearrange("p (half c) -> p half c", half=2)[:, half],
                 op0=ALU.mult, op1=ALU.subtract,
             )
 
         def store(t):
-            nc.sync.dma_start(out=y_hbm[:, t, :], in_=y[t // 2][:, t % 2, :])
+            nc.sync.dma_start(out=y_hbm[:, t], in_=y[t // 2][:, :, t % 2, :])
 
-        def planes(cols):
+        def round_views(h, half):
+            return rounded[:, half, :, 2 * h : 2 * h + 2], y[h][:, half].rearrange("p half e c -> p half c e")
+
+        def planes(half):
             nc.vector.quantize_mx(
-                out=y_codes[:, cols].bitcast(FP8X4),
-                scales=y_scales[:, cols],
-                in_=rounded[:, cols, :].rearrange("p n t -> p (n t)"),
+                out=y_codes[:, half, :].bitcast(FP8X4),
+                scales=y_scales[:, half, :],
+                in_=rounded[:, half].rearrange("p c t -> p (c t)"),
             )
-            nc.sync.dma_start(out=words_hbm[:, cols], in_=y_codes[:, cols].bitcast(I32))
+            nc.sync.dma_start(out=words_hbm[:, half, :], in_=y_codes[:, half, :].bitcast(I32))
 
-        whole, left, right = slice(0, N), slice(0, N // 2), slice(N // 2, N)
-        for t in range(3):
+        for t in range(PACK):
             make_b(t)
-        invert(0)
-        make_b(3)
-        invert(1)
         common(0)
         common(1)
-        finish(0, whole)
+        finish(0, both)
         store(0)
-        invert(2)
-        finish(1, whole)
+        finish(1, both)
         store(1)
-        nc.scalar.activation(out=rounded[:, :, 0:2], in_=y[0][:].rearrange("p e n -> p n e"), func=ACT.Copy)
+        target, source = round_views(0, both)
+        nc.scalar.activation(out=target, in_=source, func=ACT.Copy)
         common(2)
         common(3)
-        finish(2, whole)
+        finish(2, both)
         store(2)
         finish(3, left)
         finish(3, right)
         store(3)
-        last = y[1][:].rearrange("p e n -> p n e")
-        nc.scalar.activation(out=rounded[:, left, 2:4], in_=last[:, left, :], func=ACT.Copy)
-        nc.vector.tensor_copy(out=rounded[:, right, 2:4], in_=last[:, right, :])
-        planes(left)
-        planes(right)
-        for q in range(4):
+        target, source = round_views(1, left)
+        nc.scalar.activation(out=target, in_=source, func=ACT.Copy)
+        target, source = round_views(1, right)
+        nc.vector.tensor_copy(out=target, in_=source)
+        planes(0)
+        planes(1)
+        scale_rows = y_scales[:].rearrange("p half c -> p (half c)").bitcast(I32)
+        for q in range(PACK):
             queue = nc.scalar if q % 2 else nc.sync
-            queue.dma_start(
-                out=out_2[0, 4 * q : 4 * q + 4, :].bitcast(I32), in_=y_scales[32 * q : 32 * q + 4, :].bitcast(I32)
-            )
+            queue.dma_start(out=out_2[0, 4 * q : 4 * q + 4, :].bitcast(I32), in_=scale_rows[32 * q : 32 * q + 4, :])

@@ -88,15 +88,13 @@ def tile_moe_expert_less_common_part_pl_kernel(
 
         wa_scale = load_scales("wa_scale", wa_scales)
         wa = [load_wa(0)]
-        wb_scale = load_scales("wb_scale", wb_scales)
         wb = [load_wb(0)]
+        wb_scale = load_scales("wb_scale", wb_scales)
         wa.append(load_wa(1))
         wb.append(load_wb(1))
 
         ident = keep.tile([P, P], F32, name="ident")
         make_identity(nc, ident[:])
-        minus_one = keep.tile([P, 2], F32, name="minus_one")
-        nc.gpsimd.memset(minus_one[:], -1.0)
 
         spread = bank("a0", "spread")
         for c in range(PACK):
@@ -244,9 +242,9 @@ def tile_moe_expert_less_common_part_pl_kernel(
             nc.scalar.activation(out=squares[:], in_=b_rows[t][:], func=ACT.Square, accum_out=sums[h][:, i : i + 1])
             if t == GROUPS[h][-1]:
                 nc.scalar.activation(out=denominators[h][:], in_=sums[h][:], func=ACT.Copy, bias=0.1 * N, scale=1.0)
-                nc.gpsimd.tensor_tensor(
-                    out=inverses[h][:], in0=denominators[h][:], in1=minus_one[:, 0 : i + 1], op=ALU.pow
-                )
+
+        def invert(h):
+            nc.vector.reciprocal(out=inverses[h][:], in_=denominators[h][:])
 
         def common(t):
             h, i = place[t]
@@ -279,12 +277,16 @@ def tile_moe_expert_less_common_part_pl_kernel(
             )
             nc.sync.dma_start(out=words_hbm[:, half, :], in_=y_codes[:, half, :].bitcast(I32))
 
-        for t in range(PACK):
+        for t in range(PACK - 1):
             make_b(t)
+        invert(0)
+        make_b(PACK - 1)
+        invert(1)
         common(0)
         common(1)
         finish(0, both)
         store(0)
+        invert(2)
         finish(1, both)
         store(1)
         target, source = round_views(0, both)

from contextlib import ExitStack

import concourse.mybir as mybir
from concourse.masks import make_identity

K, T, J, N = 1024, 2048, 512, 512
FLOPS = 2 * 2 * K * J * N

F32 = mybir.dt.float32
BF16 = mybir.dt.bfloat16
I32 = mybir.dt.int32
U32 = mybir.dt.uint32
U16 = mybir.dt.uint16
U8 = mybir.dt.uint8
FP8X4 = mybir.dt.float8_e4m3fn_x4
FP4X4 = mybir.dt.float4_e2m1fn_x4
ACT = mybir.ActivationFunctionType
ALU = mybir.AluOpType

P = 128
PACK = 4
PASSES = K // (P * PACK)
A, B = 0, 1
BANK = 512


def two_thirds(tokens):
    return 2 * tokens // 3 // 32 * 32


LOADS = (
    ((T, two_thirds(T)),),
    ((T // 2, 0), (T // 2, two_thirds(T // 2))),
    ((T // 4, 0), (T // 4, 0), (T // 2, T // 4)),
    ((T // 2, 0), (T // 4, T // 4), (T // 4, two_thirds(T // 4))),
)
GROUPS = ((0,), (1,), (2, 3))


def tile_moe_expert_less_common_part_pl_kernel(
    tc, xt, wa_words, wa_scales, wb_words, wb_scales, bi, offs, offs2, out_0, out_1, out_2
):
    nc = tc.nc
    with ExitStack() as ctx:
        keep = ctx.enter_context(tc.tile_pool(name="keep", bufs=1))
        psum = ctx.enter_context(tc.psum_pool(name="psum", bufs=1))

        def bank(tag, name):
            return psum.tile([P, BANK], F32, name=name, tag=tag)

        bias_four = keep.tile([P, PACK], F32, name="bias_four")
        nc.scalar.dma_start(out=bias_four[:], in_=bi.rearrange("o (p c) -> (o p) c", c=PACK))

        x_pairs = xt.rearrange("(g p u e) t -> g u p e t", g=PASSES, p=P, u=2, e=2)
        raw, lists = {}, []
        for pair, loads in enumerate(LOADS):
            first = 0
            for i, (tokens, on_vector) in enumerate(loads):
                piece = keep.tile([P, 2, tokens], F32, name=f"raw{pair}_{i}", align_bytes=64)
                nc.sync.dma_start(out=piece[:], in_=x_pairs[pair // 2, pair % 2, :, :, first : first + tokens])
                raw[pair, i] = (piece, first, tokens, on_vector)
                first = first + tokens
            if pair == 0:
                for name, source in (("list_a", offs), ("list_b", offs2)):
                    entries = keep.tile([P, J // 16], U16, name=name)
                    nc.sync.dma_start(entries[:], source)
                    lists.append(entries)

        def load_scales(name, source):
            tile = keep.tile([P, PASSES, N], U8, name=name, align_bytes=64)
            nc.vector.memset(tile[:].rearrange("p g n -> p (g n)").bitcast(I32), 0)
            for q in range(PACK):
                nc.sync.dma_start(
                    out=tile[32 * q : 32 * q + 4].bitcast(I32),
                    in_=source[:, 4 * q : 4 * q + 4, :].rearrange("g r n -> r g n").bitcast(I32),
                )
            return tile

        def load_wa(g):
            tile = keep.tile([P, 2 * N], U8, name=f"wa{g}", align_bytes=64)
            nc.sync.dma_start(out=tile[:].bitcast(I32), in_=wa_words[g].bitcast(I32))
            return tile

        def load_wb(g):
            tile = keep.tile([P, N], I32, name=f"wb{g}", align_bytes=64)
            nc.sync.dma_start(out=tile[:], in_=wb_words[g].rearrange("p n r -> p (n r)").bitcast(I32))
            return tile

        wa_scale = load_scales("wa_scale", wa_scales)
        wa = [load_wa(0)]
        wb = [load_wb(0)]
        wb_scale = load_scales("wb_scale", wb_scales)
        wa.append(load_wa(1))
        wb.append(load_wb(1))

        ident = keep.tile([P, P], F32, name="ident")
        make_identity(nc, ident[:])

        spread = bank("a0", "spread")
        for c in range(PACK):
            nc.tensor.transpose(spread[:, c * P : (c + 1) * P], bias_four[:, c : c + 1].to_broadcast([P, P]), ident[:])
        bias_rows = keep.tile([P, N], F32, name="bias_rows")
        nc.vector.tensor_copy(
            out=bias_rows[:].rearrange("p (m c) -> p m c", c=PACK), in_=spread[:].rearrange("p (c m) -> p m c", c=PACK)
        )
        upright = bank("a1", "upright")
        for nb in range(PACK):
            nc.tensor.transpose(upright[:, nb * P : (nb + 1) * P], bias_rows[:, nb * P : (nb + 1) * P], ident[:])
        neg_bias_cols = keep.tile([P, PACK], F32, name="neg_bias_cols")
        nc.vector.tensor_scalar(out=neg_bias_cols[:], in0=upright[:, 0:N:P], scalar1=-1.0, scalar2=None, op0=ALU.mult)

        a_turned = [bank(f"a{nb}", f"a_turned{nb}") for nb in range(PACK)]
        b_sums = [bank(f"b{t}", f"b_sums{t}") for t in range(PACK)]
        windows = [keep.tile([P, T, 2], BF16, name=f"window{pair}") for pair in range(len(LOADS))]
        wholes = [(s, 0, J) for s in (A, B)]
        halves = [(s, j0, j0 + J // 2) for s in (A, B) for j0 in (0, J // 2)]
        picked = {
            (g, s, j0): keep.tile([P, 2, j1 - j0], U32, name=f"picked{g}_{s}_{j0}")
            for g, parts in enumerate((wholes, halves))
            for s, j0, j1 in parts
        }
        woven = {}
        operands = [(g, s) for g in range(PASSES) for s in (A, B)]
        codes = {(g, s): keep.tile([P, J], U32, name=f"codes{g}_{s}", align_bytes=64) for g, s in operands}
        scales = {(g, s): keep.tile([P, J], U8, name=f"scales{g}_{s}", align_bytes=64) for g, s in operands}

        def cast(pair, i):
            piece, first, tokens, on_vector = raw[pair, i]
            by_token = piece[:].rearrange("p e t -> p t e")
            target = windows[pair][:, first : first + tokens, :]
            if on_vector > 0:
                nc.vector.tensor_copy(out=target[:, 0:on_vector, :], in_=by_token[:, 0:on_vector, :])
            if on_vector < tokens:
                nc.scalar.activation(out=target[:, on_vector:, :], in_=by_token[:, on_vector:, :], func=ACT.Copy)

        def gather(pair, s, j0, j1):
            words = windows[pair][:].rearrange("p t e -> p (t e)").bitcast(U32)
            nc.vector.tensor_copy(
                out=picked[pair // 2, s, j0][:, pair % 2, :], in_=words.indirect(lists[s][:, j0 // 16 : j1 // 16])
            )

        def weave_views(g, s, j0, j1):
            target = woven[g, s][:].bitcast(U32).rearrange("p (t m u) -> p m u t", t=PACK, u=2)
            return target[:, j0 // PACK : j1 // PACK], picked[g, s, j0][:].rearrange("p u (m t) -> p m u t", t=PACK)

        def quantise(g, s):
            nc.vector.quantize_mx(out=codes[g, s][:].bitcast(FP8X4), scales=scales[g, s][:], in_=woven[g, s][:])

        def multiply_a(g, blocks):
            for nb in blocks:
                nc.tensor.matmul_mx(
                    out=a_turned[nb][:],
                    lhsT=wa[g][:, 2 * P * nb : 2 * P * (nb + 1)].bitcast(FP4X4),
                    lhsT_scale=wa_scale[:, g, P * nb : P * (nb + 1)],
                    rhs=codes[g, A][:].bitcast(FP8X4),
                    rhs_scale=scales[g, A][:],
                    start=(g == 0),
                    stop=(g == PASSES - 1),
                )

        def multiply_b(g, tiles):
            for t in tiles:
                nc.tensor.matmul_mx(
                    out=b_sums[t][:],
                    lhsT=codes[g, B][:, P * t : P * (t + 1)].bitcast(FP8X4),
                    lhsT_scale=scales[g, B][:, P * t : P * (t + 1)],
                    rhs=wb[g][:].bitcast(FP8X4),
                    rhs_scale=wb_scale[:, g, :],
                    start=(g == 0),
                    stop=(g == PASSES - 1),
                )

        for pair in (0, 1):
            for i in range(len(LOADS[pair])):
                cast(pair, i)
            for part in wholes:
                gather(pair, *part)
        cast(2, 0)
        cast(2, 1)
        woven[0, A] = keep.tile([P, PACK * J], BF16, name="woven0_0", tag="raw2_1", align_bytes=64)
        for g, s in operands[1:]:
            woven[g, s] = keep.tile([P, PACK * J], BF16, name=f"woven{g}_{s}", align_bytes=64)
        target, source = weave_views(0, *wholes[A])
        nc.scalar.copy(out=target, in_=source)
        target, source = weave_views(0, *wholes[B])
        nc.vector.tensor_copy(out=target.bitcast(I32), in_=source.bitcast(I32))
        quantise(0, B)
        cast(2, 2)
        quantise(0, A)
        for part in halves:
            gather(2, *part)
        multiply_a(0, range(PACK))
        multiply_b(0, range(PACK))
        for i in range(len(LOADS[3])):
            cast(3, i)
        for part in halves:
            gather(3, *part)
            target, source = weave_views(1, *part)
            nc.scalar.copy(out=target, in_=source)
        quantise(1, A)
        quantise(1, B)
        multiply_a(1, range(PACK - 1))
        multiply_b(1, range(1))
        multiply_a(1, range(PACK - 1, PACK))
        multiply_b(1, range(1, PACK))

        neg_a_cols = [keep.tile([P, J], F32, name=f"neg_a_cols{nb}") for nb in range(PACK)]
        nc.vector.tensor_scalar(
            out=neg_a_cols[0][:], in0=a_turned[0][:], scalar1=-1.0, scalar2=neg_bias_cols[:, 0:1],
            op0=ALU.mult, op1=ALU.add,
        )
        for nb in range(1, PACK):
            nc.scalar.activation(
                out=neg_a_cols[nb][:], in_=a_turned[nb][:], func=ACT.Identity,
                bias=neg_bias_cols[:, nb : nb + 1], scale=-1.0,
            )
        neg_a = [bank(f"a{t}", f"neg_a{t}") for t in range(PACK)]
        for t in range(PACK):
            for nb in range(PACK):
                nc.tensor.transpose(
                    neg_a[t][:, P * nb : P * (nb + 1)], neg_a_cols[nb][:, P * t : P * (t + 1)], ident[:]
                )

        b_rows = [keep.tile([P, N], F32, name=f"b_rows{t}") for t in range(PACK)]
        sums = [keep.tile([P, len(group)], F32, name=f"sums{h}") for h, group in enumerate(GROUPS)]
        denominators = [keep.tile([P, len(group)], F32, name=f"den{h}") for h, group in enumerate(GROUPS)]
        inverses = [keep.tile([P, len(group)], F32, name=f"inv{h}") for h, group in enumerate(GROUPS)]
        place = {t: (h, i) for h, group in enumerate(GROUPS) for i, t in enumerate(group)}
        neg_share = [keep.tile([P, 1], F32, name=f"neg_share{t}") for t in range(PACK)]
        y = [keep.tile([P, 2, 2, N // 2], F32, name=f"y{h}") for h in range(2)]
        y_hbm = out_0.rearrange("(p t) (half c) -> p t half c", t=PACK, half=2)
        rounded = keep.tile([P, 2, N // 2, PACK], BF16, name="rounded", align_bytes=64)
        y_codes = keep.tile([P, 2, N // 2], U32, name="y_codes", align_bytes=64)
        y_scales = keep.tile([P, 2, N // 2], U8, name="y_scales", align_bytes=64)
        words_hbm = out_1[0].rearrange("p (half c) r -> p half (c r)", half=2).bitcast(I32)
        both, left, right = slice(0, 2), slice(0, 1), slice(1, 2)

        def make_b(t):
            h, i = place[t]
            nc.vector.tensor_tensor(out=b_rows[t][:], in0=b_sums[t][:], in1=bias_rows[:], op=ALU.add)
            squares = keep.tile([P, N], F32, name=f"squares{t}")
            nc.scalar.activation(out=squares[:], in_=b_rows[t][:], func=ACT.Square, accum_out=sums[h][:, i : i + 1])
            if t == GROUPS[h][-1]:
                nc.scalar.activation(out=denominators[h][:], in_=sums[h][:], func=ACT.Copy, bias=0.1 * N, scale=1.0)

        def invert(h):
            nc.vector.reciprocal(out=inverses[h][:], in_=denominators[h][:])

        def common(t):
            h, i = place[t]
            products = keep.tile([P, N], F32, name=f"products{t}")
            nc.vector.scalar_tensor_tensor(
                out=products[:], in0=neg_a[t][:], scalar=inverses[h][:, i : i + 1], in1=b_rows[t][:],
                op0=ALU.mult, op1=ALU.mult, accum_out=neg_share[t][:],
            )

        def finish(t, half):
            nc.vector.scalar_tensor_tensor(
                out=y[t // 2][:, half, t % 2, :],
                in0=b_rows[t][:].rearrange("p (half c) -> p half c", half=2)[:, half],
                scalar=neg_share[t][:],
                in1=neg_a[t][:].rearrange("p (half c) -> p half c", half=2)[:, half],
                op0=ALU.mult, op1=ALU.subtract,
            )

        def store(t):
            nc.sync.dma_start(out=y_hbm[:, t], in_=y[t // 2][:, :, t % 2, :])

        def round_views(h, half):
            return rounded[:, half, :, 2 * h : 2 * h + 2], y[h][:, half].rearrange("p half e c -> p half c e")

        def planes(half):
            nc.vector.quantize_mx(
                out=y_codes[:, half, :].bitcast(FP8X4),
                scales=y_scales[:, half, :],
                in_=rounded[:, half].rearrange("p c t -> p (c t)"),
            )
            nc.sync.dma_start(out=words_hbm[:, half, :], in_=y_codes[:, half, :].bitcast(I32))

        for t in range(PACK - 1):
            make_b(t)
        invert(0)
        make_b(PACK - 1)
        invert(1)
        common(0)
        common(1)
        finish(0, both)
        store(0)
        invert(2)
        finish(1, both)
        store(1)
        target, source = round_views(0, both)
        nc.scalar.activation(out=target, in_=source, func=ACT.Copy)
        common(2)
        common(3)
        finish(2, both)
        store(2)
        finish(3, left)
        finish(3, right)
        store(3)
        target, source = round_views(1, left)
        nc.scalar.activation(out=target, in_=source, func=ACT.Copy)
        target, source = round_views(1, right)
        nc.vector.tensor_copy(out=target, in_=source)
        planes(0)
        planes(1)
        scale_rows = y_scales[:].rearrange("p half c -> p (half c)").bitcast(I32)
        for q in range(PACK):
            queue = nc.scalar if q % 2 else nc.sync
            queue.dma_start(out=out_2[0, 4 * q : 4 * q + 4, :].bitcast(I32), in_=scale_rows[32 * q : 32 * q + 4, :])
